import numpy as np
import ml_dtypes


def mxq(x, axis, fmt="e4m3"):
    dtype, down = {"e4m3": (ml_dtypes.float8_e4m3fn, 7), "e5m2": (ml_dtypes.float8_e5m2, 14)}[fmt]
    v = np.moveaxis(np.asarray(x, np.float32).astype(ml_dtypes.bfloat16).astype(np.float64), axis, -1)
    blocks = v.reshape(v.shape[:-1] + (-1, 32))
    amax = np.abs(blocks).max(-1, keepdims=True)
    byte = np.maximum(np.where(amax > 0, np.frexp(amax)[1] - 1 + 127, 0) - down, 1)
    scale = np.exp2(byte - 127.0)
    codes = (blocks / scale).astype(np.float32).astype(dtype).astype(np.float64)
    return np.moveaxis((codes * scale).reshape(v.shape), -1, axis)


WIDE = False


def mx_kscale(k):
    if not WIDE:
        return np.ones(k)
    levels = np.array([10, -10, 5, -5, 0])
    if k % 512:
        return np.exp2(np.random.permutation(np.resize(levels, k // 32))).repeat(32)
    a = np.empty((k // 512, 16))
    for p in range(k // 512):
        a[p, :8] = np.random.permutation(np.resize(levels, 8))
        for g in range(8):
            far = levels[np.abs(levels - a[p, g]) >= 10]
            a[p, g + 8] = far[np.random.randint(len(far))]
    return np.exp2(a.ravel()).repeat(32)


BF16 = ml_dtypes.bfloat16


def bf(x):
    return np.asarray(x, np.float32).astype(BF16)


def f64(x):
    return np.asarray(x).astype(np.float64)


E2M1 = np.array([0.0, 0.5, 1.0, 1.5, 2.0, 3.0, 4.0, 6.0, -0.0, -0.5, -1.0, -1.5, -2.0, -3.0, -4.0, -6.0])


def pack_weight(w, fmt):
    k, n = w.shape
    w = f64(bf(w)).reshape(k // 32, 32, n)
    amax = np.abs(w).max(1)
    if fmt == "e4m3":
        byte = np.frexp(amax)[1] - 1 + 127 - 7
    else:
        mant, ex = np.frexp(amax / 6.0)
        byte = np.where(mant > 0.5, ex, ex - 1) + 127
    byte = np.clip(np.where(amax > 0, byte, 1), 1, 254)
    scaled = (w * np.exp2(127.0 - byte)[:, None, :]).reshape(k, n).astype(np.float32)
    by_word = np.ascontiguousarray(scaled.reshape(k // 512, 128, 4, n).transpose(0, 1, 3, 2))
    if fmt == "e4m3":
        words = by_word.astype(ml_dtypes.float8_e4m3fn).view(np.uint8)
    else:
        c = by_word.astype(ml_dtypes.float4_e2m1fn).view(np.uint8) & 0xF
        words = c[..., 0::2] | (c[..., 1::2] << 4)
    return np.ascontiguousarray(words), np.ascontiguousarray(byte.astype(np.uint8).reshape(k // 512, 16, n))


def unpack_weight(words, scales, fmt):
    g, p, n, _ = words.shape
    if fmt == "e4m3":
        vals = np.ascontiguousarray(words).view(ml_dtypes.float8_e4m3fn).astype(np.float64)
    else:
        nib = np.empty((g, p, n, 4), np.uint8)
        nib[..., 0::2] = words & 0xF
        nib[..., 1::2] = words >> 4
        vals = E2M1[nib]
    vals = vals * np.repeat(np.exp2(scales.astype(np.float64) - 127.0), 8, axis=1)[..., None]
    return vals.transpose(0, 1, 3, 2).reshape(g * 512, n)
def pack4(w):
    words, scales = pack_weight(w, "e2m1")
    return words.reshape(words.shape[0], 128, -1), scales


def unpack4(words, scales):
    return unpack_weight(words.reshape(words.shape[0], 128, -1, 2), scales, "e2m1")


def planes(Y):
    n, m = Y.shape
    b = f64(bf(Y)).reshape(n // 32, 32, m)
    amax = np.abs(b).max(1)
    byte = np.clip(np.where(amax > 0, np.frexp(amax)[1] - 1 + 127 - 7, 1), 1, 254)
    codes = (b * np.exp2(127.0 - byte)[:, None, :]).reshape(n, m).astype(np.float32).astype(ml_dtypes.float8_e4m3fn).view(np.uint8)
    words = codes.reshape(n // 512, 128, 4, m).transpose(0, 1, 3, 2)
    return np.ascontiguousarray(words), np.ascontiguousarray(byte.astype(np.uint8).reshape(n // 512, 16, m))


T, J, K, N = 2048, 512, 512, 1024


def setup_inputs():
    u, v = mx_kscale(J), mx_kscale(K)
    t = bf(np.random.uniform(-1.0, 1.0, T))
    s = bf(np.random.uniform(-1.5, 1.0, J))
    rho = bf(np.random.standard_normal(J) * u)
    delta_words, delta_scales = pack4(np.random.standard_normal((J, N)) * (2.0 / np.sqrt(J)) / u[:, None])
    omega = bf(np.random.uniform(-3.0, 3.0, K))
    amp = bf((1.0 + 0.2 * np.random.standard_normal(K)) * v)
    beta_words, beta_scales = pack4(np.random.standard_normal((K, N)) * (1.5 / np.sqrt(K)) / v[:, None])
    return {
        "t": t,
        "s": s,
        "rho": rho,
        "delta_words": delta_words,
        "delta_scales": delta_scales,
        "omega": omega,
        "amp": amp,
        "beta_words": beta_words,
        "beta_scales": beta_scales,
    }


def hinge_features(t, s, rho):
    return rho[None, :] * np.maximum(t[:, None] - s[None, :], 0.0)


def sine_features(t, omega, amp):
    return amp[None, :] * np.sin(omega[None, :] * t[:, None])


def core(t, s, rho, delta_words, delta_scales, omega, amp, beta_words, beta_scales):
    a = hinge_features(f64(t), f64(s), f64(rho))
    trend = mxq(a, 1, "e4m3") @ unpack4(delta_words, delta_scales)
    f = sine_features(f64(t), f64(omega), f64(amp))
    season = mxq(f, 1, "e4m3") @ unpack4(beta_words, beta_scales)
    return trend * (1.0 + season)


def reference(t, s, rho, delta_words, delta_scales, omega, amp, beta_words, beta_scales):
    R_out = core(t, s, rho, delta_words, delta_scales, omega, amp, beta_words, beta_scales)
    words, scales = planes(R_out.T)
    return R_out, words, scales

@@ -1,0 +1,406 @@
+from contextlib import ExitStack
+from math import factorial
+
+import concourse.mybir as mybir
+from concourse.masks import make_identity
+
+T, J, N = 2048, 512, 1024
+FLOPS = 2 * 2 * T * J * N
+
+F32 = mybir.dt.float32
+BF16 = mybir.dt.bfloat16
+I32 = mybir.dt.int32
+U32 = mybir.dt.uint32
+U8 = mybir.dt.uint8
+E4M3X4 = mybir.dt.float8_e4m3fn_x4
+E2M1X4 = mybir.dt.float4_e2m1fn_x4
+ALU = mybir.AluOpType
+
+P = 128
+R = 12
+TILES = T // P
+PAIRS = TILES // 2
+CHUNKS = [(0, 256), (256, 256), (512, 512), (1024, 512), (1536, 512)]
+
+
+def tile_changepointtrendtimeslearnedsines_x2_kernel(
+    tc, t, s, rho, delta_words, delta_scales, omega, amp, beta_words, beta_scales, out_0, out_1, out_2
+):
+    nc = tc.nc
+    with ExitStack() as ctx:
+        keep = ctx.enter_context(tc.tile_pool(name="keep", bufs=1))
+        work = ctx.enter_context(tc.tile_pool(name="work", bufs=2))
+        psum = ctx.enter_context(tc.psum_pool(name="psum", bufs=2))
+        ctx.enter_context(tc.manual_schedule())
+
+        x = keep.tile([P, 32], BF16, name="x", align_bytes=64)
+        amp_c = keep.tile([P, 4], BF16, name="amp_c", align_bytes=64)
+        s_c = keep.tile([P, 4], BF16, name="s_c", align_bytes=64)
+        rho_c = keep.tile([P, 4], BF16, name="rho_c", align_bytes=64)
+        t_rows = keep.tile([P, T], BF16, name="t_rows", align_bytes=64)
+        dw = keep.tile([P, 2 * N], U8, name="dw", align_bytes=64)
+        bw = keep.tile([P, 2 * N], U8, name="bw", align_bytes=64)
+        ds = keep.tile([P, N], U8, name="ds", align_bytes=64)
+        bs = keep.tile([P, N], U8, name="bs", align_bytes=64)
+
+        nc.vector.memset(ds[:].bitcast(I32), 0)
+        nc.vector.memset(bs[:].bitcast(I32), 0)
+
+        nc.sync.dma_start(out=x[:, 0:16], in_=t.rearrange("(p j) -> p j", j=16))
+        nc.sync.dma_start(out=x[:, 16:20], in_=omega.rearrange("(p j) -> p j", j=4))
+        nc.scalar.dma_start(out=t_rows[:, 0:512], in_=t[0:512].partition_broadcast(P))
+        nc.sync.dma_start(out=amp_c[:], in_=amp.rearrange("(p j) -> p j", j=4))
+        nc.scalar.dma_start(out=s_c[:], in_=s.rearrange("(p j) -> p j", j=4))
+        nc.scalar.dma_start(out=rho_c[:], in_=rho.rearrange("(p j) -> p j", j=4))
+        for tile, words, plane, rows in ((dw, delta_words, ds, delta_scales), (bw, beta_words, bs, beta_scales)):
+            nc.sync.dma_start(out=tile[:].bitcast(I32), in_=words[0].bitcast(I32))
+            for q in range(4):
+                nc.sync.dma_start(
+                    out=plane[32 * q : 32 * q + 4, :].bitcast(I32), in_=rows[0, 4 * q : 4 * q + 4, :].bitcast(I32)
+                )
+            if tile is dw:
+                nc.sync.dma_start(out=t_rows[:, 512:T], in_=t[512:T].partition_broadcast(P))
+
+        ident_bf = keep.tile([P, P], BF16, name="ident_bf", align_bytes=64)
+        ident_f = keep.tile([P, P], F32, name="ident_f", align_bytes=64)
+        row_t = keep.tile([P, 16, P], BF16, name="row_t", align_bytes=64)
+        row_w = keep.tile([P, 4, P], BF16, name="row_w", align_bytes=64)
+        make_identity(nc, ident_bf[:])
+        nc.vector.memset(row_t[:, :, 9 * R : P], 0.0)
+        nc.vector.memset(row_w[:, :, 9 * R : P], 0.0)
+
+        pw = keep.tile([P, 20, R], F32, name="pw", align_bytes=64)
+        x2 = keep.tile([P, 20], F32, name="x2")
+        x4 = keep.tile([P, 20], F32, name="x4")
+        x8 = keep.tile([P, 20], F32, name="x8")
+        x16 = keep.tile([P, 20], F32, name="x16")
+        ca = keep.tile([P, 4, R], F32, name="ca", align_bytes=64)
+        xs = x[:, 0:20]
+        mul = nc.vector.tensor_mul
+        for r in range(R):
+            nc.gpsimd.tensor_scalar(
+                out=ca[:, :, r], in0=amp_c[:], scalar1=(-1.0) ** r / factorial(2 * r + 1), scalar2=1.0, op0=ALU.mult, op1=ALU.mult
+            )
+        make_identity(nc, ident_f[:])
+
+        def spread(tile, n):
+            return tile[:].unsqueeze(2).to_broadcast([P, 20, n])
+
+        mul(x2[:], xs, xs)
+        nc.vector.tensor_copy(out=pw[:, :, 0], in_=xs)
+        mul(x4[:], x2[:], x2[:])
+        mul(pw[:, :, 1], xs, x2[:])
+        mul(x8[:], x4[:], x4[:])
+        mul(pw[:, :, 2:4], pw[:, :, 0:2], spread(x4, 2))
+        mul(x16[:], x8[:], x8[:])
+        mul(pw[:, :, 4:8], pw[:, :, 0:4], spread(x8, 4))
+
+        rho_f = keep.tile([P, 4], F32, name="rho_f")
+        rho_s = keep.tile([P, 4], F32, name="rho_s")
+        nc.vector.tensor_copy(out=rho_f[:], in_=rho_c[:])
+        mul(pw[:, :, 8:12], pw[:, :, 0:4], spread(x16, 4))
+        mul(rho_s[:], rho_c[:], s_c[:])
+
+        a_codes = {}
+        a_scales = {}
+
+        def hinge_max(c):
+            lo, w = CHUNKS[c]
+            m = work.tile([P, 4, w], BF16, name="m", tag="m", align_bytes=64)
+            for j in range(4):
+                nc.vector.tensor_scalar(
+                    out=m[:, j, :], in0=t_rows[:, lo : lo + w], scalar1=s_c[:, j : j + 1], scalar2=None, op0=ALU.max
+                )
+            return m
+
+        def hinge_affine(c, m, a, j):
+            nc.vector.tensor_scalar(
+                out=a[:, j, :],
+                in0=m[:, j, :],
+                scalar1=rho_f[:, j : j + 1],
+                scalar2=rho_s[:, j : j + 1],
+                op0=ALU.mult,
+                op1=ALU.subtract,
+            )
+
+        def hinge_group(c, a, eng):
+            lo, w = CHUNKS[c]
+            g = work.tile([P, w, 4], BF16, name="g", tag="g", align_bytes=64)
+            dst = g[:].rearrange("p (c i) j -> p c j i", i=4)
+            src = a[:].rearrange("p j (c i) -> p c j i", i=4)
+            eng(out=dst, in_=src)
+            return g
+
+        def hinge_quant(c, g):
+            lo, w = CHUNKS[c]
+            codes = keep.tile([P, w], U32, name=f"a_codes{c}", align_bytes=64)
+            scales = keep.tile([P, w], U8, name=f"a_scales{c}", align_bytes=64)
+            nc.vector.quantize_mx(
+                out=codes[:].bitcast(E4M3X4), scales=scales[:], in_=g[:].rearrange("p c j -> p (c j)")
+            )
+            a_codes[c] = codes
+            a_scales[c] = scales
+
+        def a_slices(k):
+            for c, (lo, w) in enumerate(CHUNKS):
+                if lo <= k * P < lo + w:
+                    cols = slice(k * P - lo, k * P - lo + P)
+                    return a_codes[c][:, cols], a_scales[c][:, cols]
+            raise AssertionError
+
+        hi = keep.tile([P, 20, R], BF16, name="hi", align_bytes=64)
+        mid = keep.tile([P, 20, R], BF16, name="mid", align_bytes=64)
+        low = keep.tile([P, 20, R], BF16, name="low", align_bytes=64)
+        rest = keep.tile([P, 20, R], F32, name="rest", align_bytes=64)
+        m0 = hinge_max(0)
+        a0 = work.tile([P, 4, CHUNKS[0][1]], BF16, name="a", tag="a", align_bytes=64)
+        mul(pw[:, 16:20, :], pw[:, 16:20, :], ca[:])
+        hinge_affine(0, m0, a0, 0)
+        nc.vector.tensor_copy(out=hi[:], in_=pw[:])
+        hinge_affine(0, m0, a0, 1)
+        nc.vector.tensor_sub(rest[:], pw[:], hi[:])
+        hinge_affine(0, m0, a0, 2)
+        nc.vector.tensor_copy(out=mid[:], in_=rest[:])
+        hinge_affine(0, m0, a0, 3)
+        nc.vector.tensor_sub(low[:], rest[:], mid[:])
+
+        parts = (hi, mid, low)
+        rt = row_t[:, :, 0 : 9 * R].rearrange("p j (a b r) -> p j a b r", a=3, b=3)
+        rw = row_w[:, :, 0 : 9 * R].rearrange("p j (a b r) -> p j a b r", a=3, b=3)
+        g0 = hinge_group(0, a0, nc.vector.tensor_copy)
+        for i, part in enumerate(parts):
+            nc.scalar.copy(
+                out=rt[:, :, :, i, :], in_=part[:, 0:16, :].unsqueeze(2).to_broadcast([P, 16, 3, R])
+            )
+            nc.vector.tensor_copy(
+                out=rw[:, :, i, :, :], in_=part[:, 16:20, :].unsqueeze(2).to_broadcast([P, 4, 3, R])
+            )
+        hinge_quant(0, g0)
+
+        w_rows = keep.tile([P, 4, P], BF16, name="w_rows", align_bytes=64)
+        v_rows = keep.tile([P, T], BF16, name="v_rows", align_bytes=64)
+        ps_w = psum.tile([P, 4, P], BF16, name="ps_w", tag="f")
+        for j in range(4):
+            nc.tensor.transpose(ps_w[:, j, :], row_w[:, j, :], ident_bf[:])
+        nc.scalar.copy(out=w_rows[:], in_=ps_w[:])
+        ps_v = []
+        for b in range(2):
+            bank = psum.tile([P, 8, P], BF16, name="ps_v", tag="tp")
+            for j in range(8):
+                nc.tensor.transpose(bank[:, j, :], row_t[:, 8 * b + j, :], ident_bf[:])
+            ps_v.append(bank)
+
+        def spread_tokens(lo, hi_, engines):
+            for b in range(2):
+                engines[b](
+                    out=v_rows[:].rearrange("r (q j) -> r q j", j=16)[:, lo:hi_, 8 * b : 8 * b + 8],
+                    in_=ps_v[b][:, :, lo:hi_].rearrange("r j q -> r q j"),
+                )
+
+        f_codes = {}
+        f_grouped = {}
+        trend_sb = {}
+        result = {}
+        rounded = {}
+        planes = {}
+        plane_scales = [keep.tile([P, T], U8, name=f"plane_scales{g}", align_bytes=64) for g in range(2)]
+
+        def sine_mm(k):
+            bank = psum.tile([P, 4, P], F32, name="f_bank", tag="f")
+            for j in range(4):
+                nc.tensor.matmul(
+                    bank[:, j, :], lhsT=w_rows[:, j, :], rhs=v_rows[:, k * P : (k + 1) * P], start=True, stop=True
+                )
+            return bank
+
+        def sine_copy(k, bank):
+            m = k // 2
+            if k % 2 == 0:
+                f_grouped[m] = work.tile([P, 2 * P, 4], BF16, name="fg", tag="fg", bufs=3, align_bytes=64)
+            nc.scalar.copy(
+                out=f_grouped[m][:, (k % 2) * P : (k % 2 + 1) * P, :], in_=bank[:].rearrange("p j c -> p c j")
+            )
+
+        def sine_quant(m):
+            codes = work.tile([P, 2 * P], U32, name="f_codes", tag="fc", bufs=4, align_bytes=64)
+            scales = work.tile([P, 2 * P], U8, name="f_scales", tag="fs", bufs=4, align_bytes=64)
+            nc.vector.quantize_mx(
+                out=codes[:].bitcast(E4M3X4), scales=scales[:], in_=f_grouped[m][:].rearrange("p c j -> p (c j)")
+            )
+            f_codes[m] = (codes, scales)
+
+        def product(bank, codes, scales, words, plane, h):
+            nc.tensor.matmul_mx(
+                out=bank[:],
+                lhsT=codes.bitcast(E4M3X4),
+                lhsT_scale=scales,
+                rhs=words[:, N * h : N * (h + 1)].bitcast(E2M1X4),
+                rhs_scale=plane[:, 512 * h : 512 * (h + 1)],
+                start=True,
+                stop=True,
+            )
+
+        def trend_mm(k, h):
+            codes, scales = a_slices(k)
+            bank = psum.tile([P, 512], F32, name="trend_bank", tag="trend")
+            product(bank, codes, scales, dw, ds, h)
+            return bank
+
+        def trend_copy(k, h, bank):
+            if h == 0:
+                trend_sb[k] = work.tile([P, N], F32, name="trend_sb", tag="tsb", bufs=4, align_bytes=64)
+            nc.scalar.copy(out=trend_sb[k][:, 512 * h : 512 * (h + 1)], in_=bank[:])
+
+        def season_mm(k, h):
+            codes, scales = f_codes[k // 2]
+            cols = slice((k % 2) * P, (k % 2 + 1) * P)
+            bank = psum.tile([P, 512], F32, name="season_bank", tag="season")
+            product(bank, codes[:, cols], scales[:, cols], bw, bs, h)
+            return bank
+
+        def season_mul(k, h, bank):
+            if h == 0:
+                result[k] = work.tile([P, N], F32, name="result", tag="res", bufs=5, align_bytes=64)
+            cols = slice(512 * h, 512 * (h + 1))
+            nc.vector.scalar_tensor_tensor(
+                out=result[k][:, cols], in0=bank[:], scalar=1.0, in1=trend_sb[k][:, cols], op0=ALU.add, op1=ALU.mult
+            )
+
+        def store_and_round(k, eng):
+            nc.sync.dma_start(out=out_0[k * P : (k + 1) * P, :], in_=result[k][:])
+            rounded[k] = work.tile([P, N], BF16, name="rounded", tag="rnd", bufs=5, align_bytes=64)
+            if eng == "gpsimd":
+                nc.gpsimd.tensor_scalar(
+                    out=rounded[k][:], in0=result[k][:], scalar1=1.0, scalar2=1.0, op0=ALU.mult, op1=ALU.mult
+                )
+            else:
+                for h in range(2):
+                    cols = slice(512 * h, 512 * (h + 1))
+                    nc.vector.tensor_copy(out=rounded[k][:, cols], in_=result[k][:, cols])
+
+        def turn(m):
+            banks = []
+            for g in range(2):
+                bank = psum.tile([P, 2, 2, P], F32, name="tp_bank", tag="tp")
+                for i in range(2):
+                    words = rounded[2 * m + i][:].bitcast(F32)
+                    for u in range(2):
+                        nc.tensor.transpose(
+                            bank[:, i, u, :], words[:, 256 * g + u : 256 * (g + 1) : 2], ident_f[:]
+                        )
+                banks.append(bank)
+            return banks
+
+        def turn_copy(m, g, bank, eng):
+            tile = work.tile([P, 2 * P, 4], BF16, name="pl", tag="pl", bufs=4, align_bytes=64)
+            planes[m, g] = tile
+            eng(
+                out=tile[:].rearrange("p m t -> p (m t)").bitcast(F32).rearrange("p (i r u) -> p i r u", i=2, u=2),
+                in_=bank[:].rearrange("p i u r -> p i r u"),
+            )
+
+        def plane_quant(m, g):
+            codes = work.tile([P, 2 * P], U32, name="pl_codes", tag="plc", bufs=6, align_bytes=64)
+            cols = slice(2 * P * m, 2 * P * (m + 1))
+            nc.vector.quantize_mx(
+                out=codes[:].bitcast(E4M3X4),
+                scales=plane_scales[g][:, cols],
+                in_=planes[m, g][:].rearrange("p m t -> p (m t)"),
+            )
+            nc.sync.dma_start(
+                out=out_1[g].rearrange("p m t -> p (m t)").bitcast(I32)[:, cols], in_=codes[:].bitcast(I32)
+            )
+
+        def scale_stores(lo, hi_):
+            for g in range(2):
+                for q in range(4):
+                    nc.sync.dma_start(
+                        out=out_2[g, 4 * q : 4 * q + 4, lo:hi_].bitcast(I32),
+                        in_=plane_scales[g][32 * q : 32 * q + 4, lo:hi_].bitcast(I32),
+                    )
+
+        def hinge_chunk(c):
+            m = hinge_max(c)
+            a = work.tile([P, 4, CHUNKS[c][1]], BF16, name="a", tag="a", align_bytes=64)
+            for j in range(4):
+                hinge_affine(c, m, a, j)
+            return a
+
+        spread_tokens(0, 16, (nc.scalar.copy, nc.vector.tensor_copy))
+        f0 = sine_mm(0)
+        f1 = sine_mm(1)
+        tb = [trend_mm(0, 0), trend_mm(0, 1)]
+        a1 = hinge_chunk(1)
+        sine_copy(0, f0)
+        sine_copy(1, f1)
+        g1 = hinge_group(1, a1, nc.vector.tensor_copy)
+        sine_quant(0)
+        trend_copy(0, 0, tb[0])
+        trend_copy(0, 1, tb[1])
+        tb = [trend_mm(1, 0), trend_mm(1, 1)]
+        trend_copy(1, 0, tb[0])
+        trend_copy(1, 1, tb[1])
+        hinge_quant(1, g1)
+        spread_tokens(16, P, (nc.scalar.copy, nc.scalar.copy))
+        f2 = sine_mm(2)
+        f3 = sine_mm(3)
+        sine_copy(2, f2)
+        sine_copy(3, f3)
+        a2 = hinge_chunk(2)
+
+        pending = {"a": a2, "c": 2}
+
+        turned = []
+        for m in range(PAIRS):
+            for i in range(2):
+                k = 2 * m + i
+                nxt = k + 2
+                if nxt < TILES:
+                    tb0 = trend_mm(nxt, 0)
+                sb0 = season_mm(k, 0)
+                if nxt < TILES:
+                    tb1 = trend_mm(nxt, 1)
+                sb1 = season_mm(k, 1)
+                if nxt < TILES:
+                    trend_copy(nxt, 0, tb0)
+                season_mul(k, 0, sb0)
+                if k + 4 < TILES:
+                    fb = sine_mm(k + 4)
+                    sine_copy(k + 4, fb)
+                if i == 1 and m >= 1:
+                    for g, bank in enumerate(turn(m - 1)):
+                        turned.append((m - 1, g, bank))
+                if nxt < TILES:
+                    trend_copy(nxt, 1, tb1)
+                season_mul(k, 1, sb1)
+                store_and_round(k, "gpsimd" if k < TILES - 1 else "vector")
+                if turned:
+                    pm, pg, bank = turned.pop(0)
+                    turn_copy(pm, pg, bank, nc.scalar.copy)
+                    waiting = (pm, pg)
+                else:
+                    waiting = None
+                if i == 0:
+                    if m + 1 < PAIRS:
+                        sine_quant(m + 1)
+                    if pending["a"] is not None:
+                        pending["g"] = hinge_group(pending["c"], pending["a"], nc.vector.tensor_copy)
+                else:
+                    if pending["a"] is not None:
+                        hinge_quant(pending["c"], pending["g"])
+                        pending["a"] = None
+                if waiting is not None:
+                    plane_quant(*waiting)
+            if m in (1, 3):
+                pending["c"] = 3 if m == 1 else 4
+                pending["a"] = hinge_chunk(pending["c"])
+            if m == 5:
+                scale_stores(0, 1024)
+        m = PAIRS - 1
+        for g, bank in enumerate(turn(m)):
+            turned.append((m, g, bank))
+        engines = [nc.scalar.copy, nc.vector.tensor_copy, nc.scalar.copy]
+        for (pm, pg, bank), eng in zip(turned, engines):
+            turn_copy(pm, pg, bank, eng)
+            plane_quant(pm, pg)
+        scale_stores(1024, T)

@@ -78,9 +78,7 @@ def tile_changepointtrendtimeslearnedsines_x2_kernel(
         xs = x[:, 0:20]
         mul = nc.vector.tensor_mul
         for r in range(R):
-            nc.gpsimd.tensor_scalar(
-                out=ca[:, :, r], in0=amp_c[:], scalar1=(-1.0) ** r / factorial(2 * r + 1), scalar2=1.0, op0=ALU.mult, op1=ALU.mult
-            )
+            nc.scalar.mul(ca[:, :, r], amp_c[:], (-1.0) ** r / factorial(2 * r + 1))
         make_identity(nc, ident_f[:])
 
         def spread(tile, n):
@@ -178,7 +176,7 @@ def tile_changepointtrendtimeslearnedsines_x2_kernel(
         hinge_quant(0, g0)
 
         w_rows = keep.tile([P, 4, P], BF16, name="w_rows", align_bytes=64)
-        v_rows = keep.tile([P, T], BF16, name="v_rows", align_bytes=64)
+        v_rows = keep.tile([P, 16, P], BF16, name="v_rows", align_bytes=64)
         ps_w = psum.tile([P, 4, P], BF16, name="ps_w", tag="f")
         for j in range(4):
             nc.tensor.transpose(ps_w[:, j, :], row_w[:, j, :], ident_bf[:])
@@ -189,13 +187,6 @@ def tile_changepointtrendtimeslearnedsines_x2_kernel(
             for j in range(8):
                 nc.tensor.transpose(bank[:, j, :], row_t[:, 8 * b + j, :], ident_bf[:])
             ps_v.append(bank)
-
-        def spread_tokens(lo, hi_, engines):
-            for b in range(2):
-                engines[b](
-                    out=v_rows[:].rearrange("r (q j) -> r q j", j=16)[:, lo:hi_, 8 * b : 8 * b + 8],
-                    in_=ps_v[b][:, :, lo:hi_].rearrange("r j q -> r q j"),
-                )
 
         f_codes = {}
         f_grouped = {}
@@ -209,7 +200,11 @@ def tile_changepointtrendtimeslearnedsines_x2_kernel(
             bank = psum.tile([P, 4, P], F32, name="f_bank", tag="f")
             for j in range(4):
                 nc.tensor.matmul(
-                    bank[:, j, :], lhsT=w_rows[:, j, :], rhs=v_rows[:, k * P : (k + 1) * P], start=True, stop=True
+                    bank[:, j, :].rearrange("p (j q) -> p j q", j=16),
+                    lhsT=w_rows[:, j, :],
+                    rhs=v_rows[:, :, 8 * k : 8 * k + 8],
+                    start=True,
+                    stop=True,
                 )
             return bank
 
@@ -218,7 +213,8 @@ def tile_changepointtrendtimeslearnedsines_x2_kernel(
             if k % 2 == 0:
                 f_grouped[m] = work.tile([P, 2 * P, 4], BF16, name="fg", tag="fg", bufs=3, align_bytes=64)
             nc.scalar.copy(
-                out=f_grouped[m][:, (k % 2) * P : (k % 2 + 1) * P, :], in_=bank[:].rearrange("p j c -> p c j")
+                out=f_grouped[m][:, (k % 2) * P : (k % 2 + 1) * P, :].rearrange("p (q j) c -> p q j c", j=16),
+                in_=bank[:].rearrange("p c (j q) -> p q j c", j=16),
             )
 
         def sine_quant(m):
@@ -266,30 +262,27 @@ def tile_changepointtrendtimeslearnedsines_x2_kernel(
                 out=result[k][:, cols], in0=bank[:], scalar=1.0, in1=trend_sb[k][:, cols], op0=ALU.add, op1=ALU.mult
             )
 
-        def store_and_round(k, eng):
-            nc.sync.dma_start(out=out_0[k * P : (k + 1) * P, :], in_=result[k][:])
-            rounded[k] = work.tile([P, N], BF16, name="rounded", tag="rnd", bufs=5, align_bytes=64)
-            if eng == "gpsimd":
-                nc.gpsimd.tensor_scalar(
-                    out=rounded[k][:], in0=result[k][:], scalar1=1.0, scalar2=1.0, op0=ALU.mult, op1=ALU.mult
-                )
+        def round_half(k, h, on_vector):
+            if h == 0:
+                rounded[k] = work.tile([P, N], BF16, name="rounded", tag="rnd", bufs=5, align_bytes=64)
+            cols = slice(512 * h, 512 * (h + 1))
+            if on_vector:
+                nc.vector.tensor_copy(out=rounded[k][:, cols], in_=result[k][:, cols])
             else:
-                for h in range(2):
-                    cols = slice(512 * h, 512 * (h + 1))
-                    nc.vector.tensor_copy(out=rounded[k][:, cols], in_=result[k][:, cols])
+                nc.gpsimd.tensor_scalar(
+                    out=rounded[k][:, cols], in0=result[k][:, cols], scalar1=1.0, scalar2=1.0, op0=ALU.mult, op1=ALU.mult
+                )
 
-        def turn(m):
-            banks = []
-            for g in range(2):
-                bank = psum.tile([P, 2, 2, P], F32, name="tp_bank", tag="tp")
-                for i in range(2):
-                    words = rounded[2 * m + i][:].bitcast(F32)
-                    for u in range(2):
-                        nc.tensor.transpose(
-                            bank[:, i, u, :], words[:, 256 * g + u : 256 * (g + 1) : 2], ident_f[:]
-                        )
-                banks.append(bank)
-            return banks
+        def store(k):
+            nc.sync.dma_start(out=out_0[k * P : (k + 1) * P, :], in_=result[k][:])
+
+        def turn(m, g):
+            bank = psum.tile([P, 2, 2, P], F32, name="tp_bank", tag="tp")
+            for i in range(2):
+                words = rounded[2 * m + i][:].bitcast(F32)
+                for u in range(2):
+                    nc.tensor.transpose(bank[:, i, u, :], words[:, 256 * g + u : 256 * (g + 1) : 2], ident_f[:])
+            return bank
 
         def turn_copy(m, g, bank, eng):
             tile = work.tile([P, 2 * P, 4], BF16, name="pl", tag="pl", bufs=4, align_bytes=64)
@@ -319,88 +312,90 @@ def tile_changepointtrendtimeslearnedsines_x2_kernel(
                         in_=plane_scales[g][32 * q : 32 * q + 4, lo:hi_].bitcast(I32),
                     )
 
-        def hinge_chunk(c):
-            m = hinge_max(c)
-            a = work.tile([P, 4, CHUNKS[c][1]], BF16, name="a", tag="a", align_bytes=64)
-            for j in range(4):
-                hinge_affine(c, m, a, j)
-            return a
+        stage = {}
 
-        spread_tokens(0, 16, (nc.scalar.copy, nc.vector.tensor_copy))
+        def hinge_piece(c, piece):
+            if piece == 0:
+                stage[c] = hinge_max(c)
+            elif piece == 1:
+                a = work.tile([P, 4, CHUNKS[c][1]], BF16, name="a", tag="a", align_bytes=64)
+                for j in range(4):
+                    hinge_affine(c, stage[c], a, j)
+                stage[c] = a
+            elif piece == 2:
+                stage[c] = hinge_group(c, stage[c], nc.vector.tensor_copy)
+            else:
+                hinge_quant(c, stage[c])
+
+        nc.scalar.copy(out=v_rows[:, 0:8, :], in_=ps_v[0][:])
+        nc.vector.tensor_copy(out=v_rows[:, 8:16, :], in_=ps_v[1][:])
+        tb = [trend_mm(0, 0), trend_mm(0, 1)]
         f0 = sine_mm(0)
         f1 = sine_mm(1)
-        tb = [trend_mm(0, 0), trend_mm(0, 1)]
-        a1 = hinge_chunk(1)
+        hinge_piece(1, 0)
+        hinge_piece(1, 1)
         sine_copy(0, f0)
         sine_copy(1, f1)
-        g1 = hinge_group(1, a1, nc.vector.tensor_copy)
+        hinge_piece(1, 2)
         sine_quant(0)
+        hinge_piece(1, 3)
         trend_copy(0, 0, tb[0])
         trend_copy(0, 1, tb[1])
         tb = [trend_mm(1, 0), trend_mm(1, 1)]
-        trend_copy(1, 0, tb[0])
-        trend_copy(1, 1, tb[1])
-        hinge_quant(1, g1)
-        spread_tokens(16, P, (nc.scalar.copy, nc.scalar.copy))
         f2 = sine_mm(2)
         f3 = sine_mm(3)
+        trend_copy(1, 0, tb[0])
+        trend_copy(1, 1, tb[1])
         sine_copy(2, f2)
         sine_copy(3, f3)
-        a2 = hinge_chunk(2)
+        hinge_piece(2, 0)
+        hinge_piece(2, 1)
+        hinge_piece(2, 2)
 
-        pending = {"a": a2, "c": 2}
-
+        hinge_plan = {0: (2, 3), 1: (3, 0), 2: (3, 1), 3: (3, 2), 4: (3, 3), 5: (4, 0), 6: (4, 1), 7: (4, 2), 8: (4, 3)}
         turned = []
-        for m in range(PAIRS):
-            for i in range(2):
-                k = 2 * m + i
-                nxt = k + 2
-                if nxt < TILES:
-                    tb0 = trend_mm(nxt, 0)
-                sb0 = season_mm(k, 0)
-                if nxt < TILES:
-                    tb1 = trend_mm(nxt, 1)
-                sb1 = season_mm(k, 1)
-                if nxt < TILES:
-                    trend_copy(nxt, 0, tb0)
-                season_mul(k, 0, sb0)
-                if k + 4 < TILES:
-                    fb = sine_mm(k + 4)
-                    sine_copy(k + 4, fb)
-                if i == 1 and m >= 1:
-                    for g, bank in enumerate(turn(m - 1)):
-                        turned.append((m - 1, g, bank))
-                if nxt < TILES:
-                    trend_copy(nxt, 1, tb1)
-                season_mul(k, 1, sb1)
-                store_and_round(k, "gpsimd" if k < TILES - 1 else "vector")
-                if turned:
-                    pm, pg, bank = turned.pop(0)
-                    turn_copy(pm, pg, bank, nc.scalar.copy)
-                    waiting = (pm, pg)
-                else:
-                    waiting = None
-                if i == 0:
-                    if m + 1 < PAIRS:
-                        sine_quant(m + 1)
-                    if pending["a"] is not None:
-                        pending["g"] = hinge_group(pending["c"], pending["a"], nc.vector.tensor_copy)
-                else:
-                    if pending["a"] is not None:
-                        hinge_quant(pending["c"], pending["g"])
-                        pending["a"] = None
-                if waiting is not None:
-                    plane_quant(*waiting)
-            if m in (1, 3):
-                pending["c"] = 3 if m == 1 else 4
-                pending["a"] = hinge_chunk(pending["c"])
-            if m == 5:
+        quants = []
+        for k in range(TILES):
+            nxt = k + 2
+            sb0 = season_mm(k, 0)
+            if nxt < TILES:
+                tb0 = trend_mm(nxt, 0)
+            sb1 = season_mm(k, 1)
+            if nxt < TILES:
+                tb1 = trend_mm(nxt, 1)
+            if k + 4 < TILES:
+                fb = sine_mm(k + 4)
+            season_mul(k, 0, sb0)
+            round_half(k, 0, k == TILES - 1)
+            season_mul(k, 1, sb1)
+            round_half(k, 1, k == TILES - 1)
+            store(k)
+            if nxt < TILES:
+                trend_copy(nxt, 0, tb0)
+            if k + 4 < TILES:
+                sine_copy(k + 4, fb)
+            if nxt < TILES:
+                trend_copy(nxt, 1, tb1)
+            if k % 2 == 0 and k >= 2:
+                m = k // 2 - 1
+                turned = [(m, g, turn(m, g)) for g in range(2)]
+            if turned:
+                m, g, bank = turned.pop(0)
+                turn_copy(m, g, bank, nc.scalar.copy)
+                quants.append((m, g))
+            if k % 2 == 0 and k + 2 < TILES:
+                sine_quant(k // 2 + 1)
+            if len(quants) > 1:
+                plane_quant(*quants.pop(0))
+            if k in hinge_plan:
+                hinge_piece(*hinge_plan[k])
+            if k == 11:
                 scale_stores(0, 1024)
+        for item in quants:
+            plane_quant(*item)
         m = PAIRS - 1
-        for g, bank in enumerate(turn(m)):
-            turned.append((m, g, bank))
-        engines = [nc.scalar.copy, nc.vector.tensor_copy, nc.scalar.copy]
-        for (pm, pg, bank), eng in zip(turned, engines):
-            turn_copy(pm, pg, bank, eng)
-            plane_quant(pm, pg)
+        for g in range(2):
+            bank = turn(m, g)
+            turn_copy(m, g, bank, nc.scalar.copy)
+            plane_quant(m, g)
         scale_stores(1024, T)

@@ -31,7 +31,6 @@ def tile_changepointtrendtimeslearnedsines_x2_kernel(
         keep = ctx.enter_context(tc.tile_pool(name="keep", bufs=1))
         work = ctx.enter_context(tc.tile_pool(name="work", bufs=2))
         psum = ctx.enter_context(tc.psum_pool(name="psum", bufs=2))
-        ctx.enter_context(tc.manual_schedule())
 
         x = keep.tile([P, 32], BF16, name="x", align_bytes=64)
         amp_c = keep.tile([P, 4], BF16, name="amp_c", align_bytes=64)
@@ -196,24 +195,22 @@ def tile_changepointtrendtimeslearnedsines_x2_kernel(
         planes = {}
         plane_scales = [keep.tile([P, T], U8, name=f"plane_scales{g}", align_bytes=64) for g in range(2)]
 
-        def sine_mm(k):
-            bank = psum.tile([P, 4, P], F32, name="f_bank", tag="f")
-            for j in range(4):
+        def sine_mm(m):
+            bank = psum.tile([P, 4, 2 * P], BF16, name="f_bank", tag="f")
+            for c in range(4):
                 nc.tensor.matmul(
-                    bank[:, j, :].rearrange("p (j q) -> p j q", j=16),
-                    lhsT=w_rows[:, j, :],
-                    rhs=v_rows[:, :, 8 * k : 8 * k + 8],
+                    bank[:, c, :].rearrange("p (j q) -> p j q", j=16),
+                    lhsT=w_rows[:, c, :],
+                    rhs=v_rows[:, :, 16 * m : 16 * m + 16],
                     start=True,
                     stop=True,
                 )
             return bank
 
-        def sine_copy(k, bank):
-            m = k // 2
-            if k % 2 == 0:
-                f_grouped[m] = work.tile([P, 2 * P, 4], BF16, name="fg", tag="fg", bufs=3, align_bytes=64)
+        def sine_copy(m, bank):
+            f_grouped[m] = work.tile([P, 2 * P, 4], BF16, name="fg", tag="fg", bufs=4, align_bytes=64)
             nc.scalar.copy(
-                out=f_grouped[m][:, (k % 2) * P : (k % 2 + 1) * P, :].rearrange("p (q j) c -> p q j c", j=16),
+                out=f_grouped[m][:].rearrange("p (q j) c -> p q j c", j=16),
                 in_=bank[:].rearrange("p c (j q) -> p q j c", j=16),
             )
 
@@ -266,12 +263,12 @@ def tile_changepointtrendtimeslearnedsines_x2_kernel(
             if h == 0:
                 rounded[k] = work.tile([P, N], BF16, name="rounded", tag="rnd", bufs=5, align_bytes=64)
             cols = slice(512 * h, 512 * (h + 1))
+            dst = rounded[k][:, cols].rearrange("p (u m e) -> p u m e", u=2, e=2)
+            src = result[k][:, cols].rearrange("p (m u e) -> p u m e", u=2, e=2)
             if on_vector:
-                nc.vector.tensor_copy(out=rounded[k][:, cols], in_=result[k][:, cols])
+                nc.vector.tensor_copy(out=dst, in_=src)
             else:
-                nc.gpsimd.tensor_scalar(
-                    out=rounded[k][:, cols], in0=result[k][:, cols], scalar1=1.0, scalar2=1.0, op0=ALU.mult, op1=ALU.mult
-                )
+                nc.gpsimd.tensor_scalar(out=dst, in0=src, scalar1=1.0, scalar2=1.0, op0=ALU.mult, op1=ALU.mult)
 
         def store(k):
             nc.sync.dma_start(out=out_0[k * P : (k + 1) * P, :], in_=result[k][:])
@@ -281,7 +278,9 @@ def tile_changepointtrendtimeslearnedsines_x2_kernel(
             for i in range(2):
                 words = rounded[2 * m + i][:].bitcast(F32)
                 for u in range(2):
-                    nc.tensor.transpose(bank[:, i, u, :], words[:, 256 * g + u : 256 * (g + 1) : 2], ident_f[:])
+                    nc.tensor.transpose(
+                        bank[:, i, u, :], words[:, 256 * g + P * u : 256 * g + P * (u + 1)], ident_f[:]
+                    )
             return bank
 
         def turn_copy(m, g, bank, eng):
@@ -323,7 +322,7 @@ def tile_changepointtrendtimeslearnedsines_x2_kernel(
                     hinge_affine(c, stage[c], a, j)
                 stage[c] = a
             elif piece == 2:
-                stage[c] = hinge_group(c, stage[c], nc.vector.tensor_copy)
+                stage[c] = hinge_group(c, stage[c], nc.scalar.copy if c == 2 else nc.vector.tensor_copy)
             else:
                 hinge_quant(c, stage[c])
 
@@ -331,23 +330,19 @@ def tile_changepointtrendtimeslearnedsines_x2_kernel(
         nc.vector.tensor_copy(out=v_rows[:, 8:16, :], in_=ps_v[1][:])
         tb = [trend_mm(0, 0), trend_mm(0, 1)]
         f0 = sine_mm(0)
-        f1 = sine_mm(1)
         hinge_piece(1, 0)
         hinge_piece(1, 1)
         sine_copy(0, f0)
-        sine_copy(1, f1)
         hinge_piece(1, 2)
         sine_quant(0)
         hinge_piece(1, 3)
         trend_copy(0, 0, tb[0])
         trend_copy(0, 1, tb[1])
         tb = [trend_mm(1, 0), trend_mm(1, 1)]
-        f2 = sine_mm(2)
-        f3 = sine_mm(3)
+        f1 = sine_mm(1)
         trend_copy(1, 0, tb[0])
         trend_copy(1, 1, tb[1])
-        sine_copy(2, f2)
-        sine_copy(3, f3)
+        sine_copy(1, f1)
         hinge_piece(2, 0)
         hinge_piece(2, 1)
         hinge_piece(2, 2)
@@ -363,8 +358,8 @@ def tile_changepointtrendtimeslearnedsines_x2_kernel(
             sb1 = season_mm(k, 1)
             if nxt < TILES:
                 tb1 = trend_mm(nxt, 1)
-            if k + 4 < TILES:
-                fb = sine_mm(k + 4)
+            if k % 2 == 0 and k + 4 < TILES:
+                fb = sine_mm(k // 2 + 2)
             season_mul(k, 0, sb0)
             round_half(k, 0, k == TILES - 1)
             season_mul(k, 1, sb1)
@@ -372,8 +367,8 @@ def tile_changepointtrendtimeslearnedsines_x2_kernel(
             store(k)
             if nxt < TILES:
                 trend_copy(nxt, 0, tb0)
-            if k + 4 < TILES:
-                sine_copy(k + 4, fb)
+            if k % 2 == 0 and k + 4 < TILES:
+                sine_copy(k // 2 + 2, fb)
             if nxt < TILES:
                 trend_copy(nxt, 1, tb1)
             if k % 2 == 0 and k >= 2:

from contextlib import ExitStack
from math import factorial

import concourse.mybir as mybir
from concourse.masks import make_identity

T, J, N = 2048, 512, 1024
FLOPS = 2 * 2 * T * J * N

F32 = mybir.dt.float32
BF16 = mybir.dt.bfloat16
I32 = mybir.dt.int32
U32 = mybir.dt.uint32
U8 = mybir.dt.uint8
E4M3X4 = mybir.dt.float8_e4m3fn_x4
E2M1X4 = mybir.dt.float4_e2m1fn_x4
ALU = mybir.AluOpType

P = 128
R = 12
TILES = T // P
PAIRS = TILES // 2
CHUNKS = [(0, 256), (256, 256), (512, 512), (1024, 512), (1536, 512)]


def tile_changepointtrendtimeslearnedsines_x2_kernel(
    tc, t, s, rho, delta_words, delta_scales, omega, amp, beta_words, beta_scales, out_0, out_1, out_2
):
    nc = tc.nc
    with ExitStack() as ctx:
        keep = ctx.enter_context(tc.tile_pool(name="keep", bufs=1))
        work = ctx.enter_context(tc.tile_pool(name="work", bufs=2))
        psum = ctx.enter_context(tc.psum_pool(name="psum", bufs=2))

        x = keep.tile([P, 32], BF16, name="x", align_bytes=64)
        amp_c = keep.tile([P, 4], BF16, name="amp_c", align_bytes=64)
        s_c = keep.tile([P, 4], BF16, name="s_c", align_bytes=64)
        rho_c = keep.tile([P, 4], BF16, name="rho_c", align_bytes=64)
        t_rows = keep.tile([P, T], BF16, name="t_rows", align_bytes=64)
        dw = keep.tile([P, 2 * N], U8, name="dw", align_bytes=64)
        bw = keep.tile([P, 2 * N], U8, name="bw", align_bytes=64)
        ds = keep.tile([P, N], U8, name="ds", align_bytes=64)
        bs = keep.tile([P, N], U8, name="bs", align_bytes=64)

        nc.vector.memset(ds[:].bitcast(I32), 0)
        nc.vector.memset(bs[:].bitcast(I32), 0)

        nc.sync.dma_start(out=x[:, 0:16], in_=t.rearrange("(p j) -> p j", j=16))
        nc.sync.dma_start(out=x[:, 16:20], in_=omega.rearrange("(p j) -> p j", j=4))
        nc.scalar.dma_start(out=t_rows[:, 0:512], in_=t[0:512].partition_broadcast(P))
        nc.sync.dma_start(out=amp_c[:], in_=amp.rearrange("(p j) -> p j", j=4))
        nc.scalar.dma_start(out=s_c[:], in_=s.rearrange("(p j) -> p j", j=4))
        nc.scalar.dma_start(out=rho_c[:], in_=rho.rearrange("(p j) -> p j", j=4))
        for tile, words, plane, rows in ((dw, delta_words, ds, delta_scales), (bw, beta_words, bs, beta_scales)):
            nc.sync.dma_start(out=tile[:].bitcast(I32), in_=words[0].bitcast(I32))
            for q in range(4):
                nc.sync.dma_start(
                    out=plane[32 * q : 32 * q + 4, :].bitcast(I32), in_=rows[0, 4 * q : 4 * q + 4, :].bitcast(I32)
                )
            if tile is dw:
                nc.sync.dma_start(out=t_rows[:, 512:T], in_=t[512:T].partition_broadcast(P))

        ident_bf = keep.tile([P, P], BF16, name="ident_bf", align_bytes=64)
        ident_f = keep.tile([P, P], F32, name="ident_f", align_bytes=64)
        row_t = keep.tile([P, 16, P], BF16, name="row_t", align_bytes=64)
        row_w = keep.tile([P, 4, P], BF16, name="row_w", align_bytes=64)
        make_identity(nc, ident_bf[:])
        nc.vector.memset(row_t[:, :, 9 * R : P], 0.0)
        nc.vector.memset(row_w[:, :, 9 * R : P], 0.0)

        pw = keep.tile([P, 20, R], F32, name="pw", align_bytes=64)
        x2 = keep.tile([P, 20], F32, name="x2")
        x4 = keep.tile([P, 20], F32, name="x4")
        x8 = keep.tile([P, 20], F32, name="x8")
        x16 = keep.tile([P, 20], F32, name="x16")
        ca = keep.tile([P, 4, R], F32, name="ca", align_bytes=64)
        xs = x[:, 0:20]
        mul = nc.vector.tensor_mul
        for r in range(R):
            nc.scalar.mul(ca[:, :, r], amp_c[:], (-1.0) ** r / factorial(2 * r + 1))
        make_identity(nc, ident_f[:])

        def spread(tile, n):
            return tile[:].unsqueeze(2).to_broadcast([P, 20, n])

        mul(x2[:], xs, xs)
        nc.vector.tensor_copy(out=pw[:, :, 0], in_=xs)
        mul(x4[:], x2[:], x2[:])
        mul(pw[:, :, 1], xs, x2[:])
        mul(x8[:], x4[:], x4[:])
        mul(pw[:, :, 2:4], pw[:, :, 0:2], spread(x4, 2))
        mul(x16[:], x8[:], x8[:])
        mul(pw[:, :, 4:8], pw[:, :, 0:4], spread(x8, 4))

        rho_f = keep.tile([P, 4], F32, name="rho_f")
        rho_s = keep.tile([P, 4], F32, name="rho_s")
        nc.vector.tensor_copy(out=rho_f[:], in_=rho_c[:])
        mul(pw[:, :, 8:12], pw[:, :, 0:4], spread(x16, 4))
        mul(rho_s[:], rho_c[:], s_c[:])

        a_codes = {}
        a_scales = {}

        def hinge_max(c):
            lo, w = CHUNKS[c]
            m = work.tile([P, 4, w], BF16, name="m", tag="m", align_bytes=64)
            for j in range(4):
                nc.vector.tensor_scalar(
                    out=m[:, j, :], in0=t_rows[:, lo : lo + w], scalar1=s_c[:, j : j + 1], scalar2=None, op0=ALU.max
                )
            return m

        def hinge_affine(c, m, a, j):
            nc.vector.tensor_scalar(
                out=a[:, j, :],
                in0=m[:, j, :],
                scalar1=rho_f[:, j : j + 1],
                scalar2=rho_s[:, j : j + 1],
                op0=ALU.mult,
                op1=ALU.subtract,
            )

        def hinge_group(c, a, eng):
            lo, w = CHUNKS[c]
            g = work.tile([P, w, 4], BF16, name="g", tag="g", align_bytes=64)
            dst = g[:].rearrange("p (c i) j -> p c j i", i=4)
            src = a[:].rearrange("p j (c i) -> p c j i", i=4)
            eng(out=dst, in_=src)
            return g

        def hinge_quant(c, g):
            lo, w = CHUNKS[c]
            codes = keep.tile([P, w], U32, name=f"a_codes{c}", align_bytes=64)
            scales = keep.tile([P, w], U8, name=f"a_scales{c}", align_bytes=64)
            nc.vector.quantize_mx(
                out=codes[:].bitcast(E4M3X4), scales=scales[:], in_=g[:].rearrange("p c j -> p (c j)")
            )
            a_codes[c] = codes
            a_scales[c] = scales

        def a_slices(k):
            for c, (lo, w) in enumerate(CHUNKS):
                if lo <= k * P < lo + w:
                    cols = slice(k * P - lo, k * P - lo + P)
                    return a_codes[c][:, cols], a_scales[c][:, cols]
            raise AssertionError

        hi = keep.tile([P, 20, R], BF16, name="hi", align_bytes=64)
        mid = keep.tile([P, 20, R], BF16, name="mid", align_bytes=64)
        low = keep.tile([P, 20, R], BF16, name="low", align_bytes=64)
        rest = keep.tile([P, 20, R], F32, name="rest", align_bytes=64)
        m0 = hinge_max(0)
        a0 = work.tile([P, 4, CHUNKS[0][1]], BF16, name="a", tag="a", align_bytes=64)
        mul(pw[:, 16:20, :], pw[:, 16:20, :], ca[:])
        hinge_affine(0, m0, a0, 0)
        nc.vector.tensor_copy(out=hi[:], in_=pw[:])
        hinge_affine(0, m0, a0, 1)
        nc.vector.tensor_sub(rest[:], pw[:], hi[:])
        hinge_affine(0, m0, a0, 2)
        nc.vector.tensor_copy(out=mid[:], in_=rest[:])
        hinge_affine(0, m0, a0, 3)
        nc.vector.tensor_sub(low[:], rest[:], mid[:])

        parts = (hi, mid, low)
        rt = row_t[:, :, 0 : 9 * R].rearrange("p j (a b r) -> p j a b r", a=3, b=3)
        rw = row_w[:, :, 0 : 9 * R].rearrange("p j (a b r) -> p j a b r", a=3, b=3)
        g0 = hinge_group(0, a0, nc.vector.tensor_copy)
        for i, part in enumerate(parts):
            nc.scalar.copy(
                out=rt[:, :, :, i, :], in_=part[:, 0:16, :].unsqueeze(2).to_broadcast([P, 16, 3, R])
            )
            nc.vector.tensor_copy(
                out=rw[:, :, i, :, :], in_=part[:, 16:20, :].unsqueeze(2).to_broadcast([P, 4, 3, R])
            )
        hinge_quant(0, g0)

        w_rows = keep.tile([P, 4, P], BF16, name="w_rows", align_bytes=64)
        v_rows = keep.tile([P, 16, P], BF16, name="v_rows", align_bytes=64)
        ps_w = psum.tile([P, 4, P], BF16, name="ps_w", tag="f")
        for j in range(4):
            nc.tensor.transpose(ps_w[:, j, :], row_w[:, j, :], ident_bf[:])
        nc.scalar.copy(out=w_rows[:], in_=ps_w[:])
        ps_v = []
        for b in range(2):
            bank = psum.tile([P, 8, P], BF16, name="ps_v", tag="tp")
            for j in range(8):
                nc.tensor.transpose(bank[:, j, :], row_t[:, 8 * b + j, :], ident_bf[:])
            ps_v.append(bank)

        f_codes = {}
        f_grouped = {}
        trend_sb = {}
        result = {}
        rounded = {}
        planes = {}
        plane_scales = [keep.tile([P, T], U8, name=f"plane_scales{g}", align_bytes=64) for g in range(2)]

        def sine_mm(m):
            bank = psum.tile([P, 4, 2 * P], BF16, name="f_bank", tag="f")
            for c in range(4):
                nc.tensor.matmul(
                    bank[:, c, :].rearrange("p (j q) -> p j q", j=16),
                    lhsT=w_rows[:, c, :],
                    rhs=v_rows[:, :, 16 * m : 16 * m + 16],
                    start=True,
                    stop=True,
                )
            return bank

        def sine_copy(m, bank):
            f_grouped[m] = work.tile([P, 2 * P, 4], BF16, name="fg", tag="fg", bufs=4, align_bytes=64)
            nc.scalar.copy(
                out=f_grouped[m][:].rearrange("p (q j) c -> p q j c", j=16),
                in_=bank[:].rearrange("p c (j q) -> p q j c", j=16),
            )

        def sine_quant(m):
            codes = work.tile([P, 2 * P], U32, name="f_codes", tag="fc", bufs=4, align_bytes=64)
            scales = work.tile([P, 2 * P], U8, name="f_scales", tag="fs", bufs=4, align_bytes=64)
            nc.vector.quantize_mx(
                out=codes[:].bitcast(E4M3X4), scales=scales[:], in_=f_grouped[m][:].rearrange("p c j -> p (c j)")
            )
            f_codes[m] = (codes, scales)

        def product(bank, codes, scales, words, plane, h):
            nc.tensor.matmul_mx(
                out=bank[:],
                lhsT=codes.bitcast(E4M3X4),
                lhsT_scale=scales,
                rhs=words[:, N * h : N * (h + 1)].bitcast(E2M1X4),
                rhs_scale=plane[:, 512 * h : 512 * (h + 1)],
                start=True,
                stop=True,
            )

        def trend_mm(k, h):
            codes, scales = a_slices(k)
            bank = psum.tile([P, 512], F32, name="trend_bank", tag="trend")
            product(bank, codes, scales, dw, ds, h)
            return bank

        def trend_copy(k, h, bank):
            if h == 0:
                trend_sb[k] = work.tile([P, N], F32, name="trend_sb", tag="tsb", bufs=4, align_bytes=64)
            nc.scalar.copy(out=trend_sb[k][:, 512 * h : 512 * (h + 1)], in_=bank[:])

        def season_mm(k, h):
            codes, scales = f_codes[k // 2]
            cols = slice((k % 2) * P, (k % 2 + 1) * P)
            bank = psum.tile([P, 512], F32, name="season_bank", tag="season")
            product(bank, codes[:, cols], scales[:, cols], bw, bs, h)
            return bank

        def season_mul(k, h, bank):
            if h == 0:
                result[k] = work.tile([P, N], F32, name="result", tag="res", bufs=5, align_bytes=64)
            cols = slice(512 * h, 512 * (h + 1))
            nc.vector.scalar_tensor_tensor(
                out=result[k][:, cols], in0=bank[:], scalar=1.0, in1=trend_sb[k][:, cols], op0=ALU.add, op1=ALU.mult
            )

        def round_half(k, h, on_vector):
            if h == 0:
                rounded[k] = work.tile([P, N], BF16, name="rounded", tag="rnd", bufs=5, align_bytes=64)
            cols = slice(512 * h, 512 * (h + 1))
            dst = rounded[k][:, cols].rearrange("p (u m e) -> p u m e", u=2, e=2)
            src = result[k][:, cols].rearrange("p (m u e) -> p u m e", u=2, e=2)
            if on_vector:
                nc.vector.tensor_copy(out=dst, in_=src)
            else:
                nc.gpsimd.tensor_scalar(out=dst, in0=src, scalar1=1.0, scalar2=1.0, op0=ALU.mult, op1=ALU.mult)

        def store(k):
            nc.sync.dma_start(out=out_0[k * P : (k + 1) * P, :], in_=result[k][:])

        def turn(m, g):
            bank = psum.tile([P, 2, 2, P], F32, name="tp_bank", tag="tp")
            for i in range(2):
                words = rounded[2 * m + i][:].bitcast(F32)
                for u in range(2):
                    nc.tensor.transpose(
                        bank[:, i, u, :], words[:, 256 * g + P * u : 256 * g + P * (u + 1)], ident_f[:]
                    )
            return bank

        def turn_copy(m, g, bank, eng):
            tile = work.tile([P, 2 * P, 4], BF16, name="pl", tag="pl", bufs=4, align_bytes=64)
            planes[m, g] = tile
            eng(
                out=tile[:].rearrange("p m t -> p (m t)").bitcast(F32).rearrange("p (i r u) -> p i r u", i=2, u=2),
                in_=bank[:].rearrange("p i u r -> p i r u"),
            )

        def plane_quant(m, g):
            codes = work.tile([P, 2 * P], U32, name="pl_codes", tag="plc", bufs=6, align_bytes=64)
            cols = slice(2 * P * m, 2 * P * (m + 1))
            nc.vector.quantize_mx(
                out=codes[:].bitcast(E4M3X4),
                scales=plane_scales[g][:, cols],
                in_=planes[m, g][:].rearrange("p m t -> p (m t)"),
            )
            nc.sync.dma_start(
                out=out_1[g].rearrange("p m t -> p (m t)").bitcast(I32)[:, cols], in_=codes[:].bitcast(I32)
            )

        def scale_stores(lo, hi_):
            for g in range(2):
                for q in range(4):
                    nc.sync.dma_start(
                        out=out_2[g, 4 * q : 4 * q + 4, lo:hi_].bitcast(I32),
                        in_=plane_scales[g][32 * q : 32 * q + 4, lo:hi_].bitcast(I32),
                    )

        stage = {}

        def hinge_piece(c, piece):
            if piece == 0:
                stage[c] = hinge_max(c)
            elif piece == 1:
                a = work.tile([P, 4, CHUNKS[c][1]], BF16, name="a", tag="a", align_bytes=64)
                for j in range(4):
                    hinge_affine(c, stage[c], a, j)
                stage[c] = a
            elif piece == 2:
                stage[c] = hinge_group(c, stage[c], nc.scalar.copy if c == 2 else nc.vector.tensor_copy)
            else:
                hinge_quant(c, stage[c])

        nc.scalar.copy(out=v_rows[:, 0:8, :], in_=ps_v[0][:])
        nc.vector.tensor_copy(out=v_rows[:, 8:16, :], in_=ps_v[1][:])
        tb = [trend_mm(0, 0), trend_mm(0, 1)]
        f0 = sine_mm(0)
        hinge_piece(1, 0)
        hinge_piece(1, 1)
        sine_copy(0, f0)
        hinge_piece(1, 2)
        sine_quant(0)
        hinge_piece(1, 3)
        trend_copy(0, 0, tb[0])
        trend_copy(0, 1, tb[1])
        tb = [trend_mm(1, 0), trend_mm(1, 1)]
        f1 = sine_mm(1)
        trend_copy(1, 0, tb[0])
        trend_copy(1, 1, tb[1])
        sine_copy(1, f1)
        hinge_piece(2, 0)
        hinge_piece(2, 1)
        hinge_piece(2, 2)

        hinge_plan = {0: (2, 3), 1: (3, 0), 2: (3, 1), 3: (3, 2), 4: (3, 3), 5: (4, 0), 6: (4, 1), 7: (4, 2), 8: (4, 3)}
        turned = []
        quants = []
        for k in range(TILES):
            nxt = k + 2
            sb0 = season_mm(k, 0)
            if nxt < TILES:
                tb0 = trend_mm(nxt, 0)
            sb1 = season_mm(k, 1)
            if nxt < TILES:
                tb1 = trend_mm(nxt, 1)
            if k % 2 == 0 and k + 4 < TILES:
                fb = sine_mm(k // 2 + 2)
            season_mul(k, 0, sb0)
            round_half(k, 0, k == TILES - 1)
            season_mul(k, 1, sb1)
            round_half(k, 1, k == TILES - 1)
            store(k)
            if nxt < TILES:
                trend_copy(nxt, 0, tb0)
            if k % 2 == 0 and k + 4 < TILES:
                sine_copy(k // 2 + 2, fb)
            if nxt < TILES:
                trend_copy(nxt, 1, tb1)
            if k % 2 == 0 and k >= 2:
                m = k // 2 - 1
                turned = [(m, g, turn(m, g)) for g in range(2)]
            if turned:
                m, g, bank = turned.pop(0)
                turn_copy(m, g, bank, nc.scalar.copy)
                quants.append((m, g))
            if k % 2 == 0 and k + 2 < TILES:
                sine_quant(k // 2 + 1)
            if len(quants) > 1:
                plane_quant(*quants.pop(0))
            if k in hinge_plan:
                hinge_piece(*hinge_plan[k])
            if k == 11:
                scale_stores(0, 1024)
        for item in quants:
            plane_quant(*item)
        m = PAIRS - 1
        for g in range(2):
            bank = turn(m, g)
            turn_copy(m, g, bank, nc.scalar.copy)
            plane_quant(m, g)
        scale_stores(1024, T)
